import numpy as np
import ml_dtypes


def mxq(x, axis, fmt="e4m3"):
    dtype, down = {"e4m3": (ml_dtypes.float8_e4m3fn, 7), "e5m2": (ml_dtypes.float8_e5m2, 14)}[fmt]
    v = np.moveaxis(np.asarray(x, np.float32).astype(ml_dtypes.bfloat16).astype(np.float64), axis, -1)
    blocks = v.reshape(v.shape[:-1] + (-1, 32))
    amax = np.abs(blocks).max(-1, keepdims=True)
    byte = np.maximum(np.where(amax > 0, np.frexp(amax)[1] - 1 + 127, 0) - down, 1)
    scale = np.exp2(byte - 127.0)
    codes = (blocks / scale).astype(np.float32).astype(dtype).astype(np.float64)
    return np.moveaxis((codes * scale).reshape(v.shape), -1, axis)


WIDE = False


def mx_kscale(k):
    if not WIDE:
        return np.ones(k)
    levels = np.array([10, -10, 5, -5, 0])
    if k % 512:
        return np.exp2(np.random.permutation(np.resize(levels, k // 32))).repeat(32)
    a = np.empty((k // 512, 16))
    for p in range(k // 512):
        a[p, :8] = np.random.permutation(np.resize(levels, 8))
        for g in range(8):
            far = levels[np.abs(levels - a[p, g]) >= 10]
            a[p, g + 8] = far[np.random.randint(len(far))]
    return np.exp2(a.ravel()).repeat(32)


def f64(x):
    return np.asarray(x).astype(np.float64)


def striped(idx):
    return np.tile(idx.reshape(-1, 16).T, (8, 1)).astype(np.uint16)


def unstriped(offs):
    return offs[:16].T.reshape(-1).astype(np.int64)


def striped8(idx):
    return np.concatenate([x.reshape(-1, 16).T for x in idx]).astype(np.uint16)


def runs(offs, k):
    lists = np.stack([offs[16 * r : 16 * r + 16].T.reshape(-1) for r in range(8)]).astype(np.int64)
    return lists[np.arange(k) % 512 // 64]


def pack_weight(w):
    k, n = w.shape
    w = f64(np.asarray(w, np.float32).astype(ml_dtypes.bfloat16)).reshape(k // 32, 32, n)
    amax = np.abs(w).max(1)
    byte = np.clip(np.where(amax > 0, np.frexp(amax)[1] - 1 + 127 - 7, 1), 1, 254)
    scaled = (w * np.exp2(127.0 - byte)[:, None, :]).reshape(k, n).astype(np.float32)
    words = np.ascontiguousarray(scaled.reshape(k // 512, 128, 4, n).transpose(0, 1, 3, 2)).astype(ml_dtypes.float8_e4m3fn).view(np.uint8)
    return words, np.ascontiguousarray(byte.astype(np.uint8).reshape(k // 512, 16, n))


def unpack_weight(words, scales):
    g, p, n, _ = words.shape
    vals = np.ascontiguousarray(words).view(ml_dtypes.float8_e4m3fn).astype(np.float64) * np.repeat(np.exp2(scales.astype(np.float64) - 127.0), 8, axis=1)[..., None]
    return vals.transpose(0, 1, 3, 2).reshape(g * 512, n)


def sigmoid(v):
    return 1.0 / (1.0 + np.exp(-np.maximum(v, -700.0)))

def planes(y):
    n, m = y.shape
    v = y.astype(np.float32).astype(ml_dtypes.bfloat16).astype(np.float64).reshape(n // 32, 32, m)
    top = np.abs(v).max(1)
    byte = np.clip(np.where(top > 0, np.frexp(top)[1] - 1 + 127 - 7, 1), 1, 254)
    codes = (v * np.exp2(127.0 - byte)[:, None, :]).reshape(n, m).astype(np.float32).astype(ml_dtypes.float8_e4m3fn).view(np.uint8)
    words = codes.reshape(n // 512, 128, 4, m).transpose(0, 1, 3, 2)
    return np.ascontiguousarray(words), np.ascontiguousarray(byte.astype(np.uint8).reshape(n // 512, 16, m))


K, T, S, H = 512, 2048, 512, 512


def setup_inputs():
    n = np.random.standard_normal
    s = mx_kscale(K)[:, None]
    u = mx_kscale(S)
    packed_xT = pack_weight(n((K, T)) * s)
    return {
        "x_words": packed_xT[0],
        "x_scales": packed_xT[1],
        "wa": (n((K, H)) / np.sqrt(K) / s).astype(np.float32),
        "wb": (n((K, H)) / np.sqrt(K) / s).astype(np.float32),
        "gt": (np.random.uniform(0.5, 1.5, (S, 1)) * u[:, None]).astype(np.float32),
        "gi": (np.random.uniform(0.5, 1.5, (S, 1)) / u[:, None]).astype(np.float32),
        "offs": striped(np.random.permutation(T)[:S]),
        "two": striped(np.random.permutation(T)[:S]),
        "n1": striped8(np.stack([np.random.permutation(H) for _ in range(8)])),
        "n2": striped8(np.stack([np.random.permutation(H) for _ in range(8)])),
        "n3": striped8(np.stack([np.random.permutation(H) for _ in range(8)])),
        "n4": striped8(np.stack([np.random.permutation(H) for _ in range(8)])),
        "n5": striped8(np.stack([np.random.permutation(H) for _ in range(8)])),
    }


def reference(x_words, x_scales, wa, wb, gt, gi, offs, two, n1, n2, n3, n4, n5):
    xq = unpack_weight(x_words, x_scales)[:, unstriped(offs)]
    a = xq.T @ mxq(f64(wa), 0, "e4m3")
    x_two = unpack_weight(x_words, x_scales)[:, unstriped(two)]
    b = x_two.T @ mxq(f64(wb), 0, "e4m3")
    z = f64(gt) * (np.maximum(a[np.arange(S)[:, None], runs(n1, S)] + b[np.arange(S)[:, None], runs(n3, S)], a[np.arange(S)[:, None], runs(n2, S)] + b[np.arange(S)[:, None], runs(n4, S)]))
    z2 = f64(gi) * b
    cv = 0.0625 * ((mxq(z, 0, "e4m3").T @ mxq(z2, 0, "e4m3")))
    out_0 = cv * (sigmoid(cv[np.arange(H)[:, None], runs(n5, H)]))
    return (out_0,) + planes(out_0)

@@ -1,0 +1,250 @@
+from contextlib import ExitStack
+
+import concourse.mybir as mybir
+from concourse.masks import make_identity
+
+K, T, S, H = 512, 2048, 512, 512
+FLOPS = 2 * K * S * H * 2 + 2 * S * H * H
+
+F32 = mybir.dt.float32
+BF16 = mybir.dt.bfloat16
+I32 = mybir.dt.int32
+U32 = mybir.dt.uint32
+U16 = mybir.dt.uint16
+U8 = mybir.dt.uint8
+FP8X4 = mybir.dt.float8_e4m3fn_x4
+ACT = mybir.ActivationFunctionType
+ALU = mybir.AluOpType
+
+P = 128
+PACK = 4
+HALF = H // 2
+CV_SCALE = 0.0625
+
+
+def tile_picked_momtpathbgate_none_po_kernel(
+    tc, x_words, x_scales, wa, wb, gt, gi, offs, two, n1, n2, n3, n4, n5, out_0, out_1, out_2
+):
+    nc = tc.nc
+    with ExitStack() as ctx:
+        lists = ctx.enter_context(tc.tile_pool(name="lists", bufs=1))
+        keep = ctx.enter_context(tc.tile_pool(name="keep", bufs=1))
+        psum = ctx.enter_context(tc.psum_pool(name="psum", bufs=1))
+
+        def sb(name, shape, dtype):
+            return keep.tile(shape, dtype, name=name, align_bytes=64)
+
+        def bank(i):
+            return psum.tile([P, H], F32, name="bank%d" % i, tag="bank%d" % i)
+
+        def load_list(name, src):
+            t = lists.tile([P, S // 16], U16, name=name)
+            nc.sync.dma_start(t[:], src)
+            return t
+
+        def entries(lst, lo, hi):
+            return lst[:, lo // 16 : hi // 16]
+
+        x_scale_table = sb("x_scale_table", [P, T], U8)
+        nc.vector.memset(x_scale_table[:].bitcast(I32), 0)
+        two_l = load_list("two_l", two)
+        offs_l = load_list("offs_l", offs)
+        for q in range(4):
+            nc.sync.dma_start(
+                x_scale_table[32 * q : 32 * q + 4, :].bitcast(I32),
+                x_scales[0, 4 * q : 4 * q + 4, :].bitcast(I32),
+            )
+        x_word_table = sb("x_word_table", [P, T], U32)
+        nc.sync.dma_start(
+            x_word_table[:].bitcast(I32),
+            x_words[0].rearrange("p n r -> p (n r)").bitcast(I32),
+        )
+
+        def load_weight(name, w):
+            halves = []
+            for h in range(2):
+                raw = sb("%s_raw%d" % (name, h), [P, PACK, HALF], F32)
+                nc.sync.dma_start(
+                    raw[:], w[:, h * HALF : (h + 1) * HALF].rearrange("(p j) c -> p j c", j=PACK)
+                )
+                halves.append(raw)
+            return halves
+
+        wb_raw = load_weight("wb", wb)
+        gate_rows = sb("gate_rows", [P, P], F32)
+        nc.gpsimd.memset(gate_rows[:], 0.0)
+        ident = sb("ident", [P, P], F32)
+        make_identity(nc, ident[:])
+        for i, g in enumerate((gt, gi)):
+            nc.sync.dma_start(
+                gate_rows[PACK * i : PACK * (i + 1), :].rearrange("t (b u) -> t b u", u=8),
+                g.rearrange("(b t u) o -> t b (u o)", t=PACK, u=8),
+            )
+        wa_raw = load_weight("wa", wa)
+        n3_l = load_list("n3_l", n3)
+        n4_l = load_list("n4_l", n4)
+        n1_l = load_list("n1_l", n1)
+        n2_l = load_list("n2_l", n2)
+        n5_l = load_list("n5_l", n5)
+
+        gate_ps = psum.tile([P, P], F32, name="gate_ps", tag="bank7")
+        nc.tensor.transpose(gate_ps[:], gate_rows[:], ident[:])
+        gt_abs = sb("gt_abs", [P, PACK], F32)
+        gt_sign = sb("gt_sign", [P, PACK], F32)
+        gi_plain = sb("gi_plain", [P, PACK], F32)
+        gi_signed = sb("gi_signed", [P, PACK], F32)
+        nc.scalar.activation(gt_abs[:], gate_ps[:, 0:PACK], ACT.Abs)
+        nc.scalar.activation(gt_sign[:], gate_ps[:, 0:PACK], ACT.Sign)
+        nc.scalar.copy(gi_plain[:], gate_ps[:, PACK : 2 * PACK])
+        nc.gpsimd.tensor_tensor(gi_signed[:], gi_plain[:], gt_sign[:], ALU.mult)
+
+        def pick_scales(name, lst):
+            picked = sb(name + "_picked", [P, S], U8)
+            nc.vector.tensor_copy(picked[:], x_scale_table[:].indirect(lst[:]))
+            dealt = sb(name, [P, S], U8)
+            nc.vector.tensor_copy(
+                dealt[:].bitcast(I32).rearrange("p (t b w) -> p t b w", t=PACK, w=2),
+                picked[:].bitcast(I32).rearrange("p (b t w) -> p t b w", t=PACK, w=2),
+            )
+            return dealt
+
+        def pick_words(name, lst):
+            dealt = sb(name, [P, S], U32)
+            nc.vector.tensor_copy(
+                dealt[:].rearrange("p (t b u) -> p b t u", t=PACK, u=8),
+                x_word_table[:].indirect(lst[:]),
+            )
+            return dealt
+
+        xb_scales = pick_scales("xb_scales", two_l)
+        xa_scales = pick_scales("xa_scales", offs_l)
+        xb_words = pick_words("xb_words", two_l)
+        xa_words = pick_words("xa_words", offs_l)
+
+        def interleave(copy, dst, src):
+            copy(
+                dst.rearrange("p (c i) t -> p c t i", i=4),
+                src.rearrange("p t (c i) -> p c t i", i=4),
+            )
+
+        def quantize(words, scales, grouped):
+            nc.vector.quantize_mx(out=words.bitcast(FP8X4), scales=scales, in_=grouped)
+
+        def quantize_weight(name, raw, copies):
+            words = sb(name + "_words", [P, H], U32)
+            scales = sb(name + "_scales", [P, H], U8)
+            grouped = [sb("%s_grouped%d" % (name, h), [P, HALF, PACK], BF16) for h in range(2)]
+            for h in range(2):
+                interleave(copies[h], grouped[h][:], raw[h][:])
+            for h in range(2):
+                cols = slice(h * HALF, (h + 1) * HALF)
+                quantize(words[:, cols], scales[:, cols], grouped[h][:].rearrange("p c t -> p (c t)"))
+            return words, scales
+
+        def product(first_bank, lhs_words, lhs_scales, rhs_words, rhs_scales):
+            banks = []
+            for t in range(PACK):
+                acc = bank(first_bank + t)
+                cols = slice(t * P, (t + 1) * P)
+                nc.tensor.matmul_mx(
+                    out=acc[:],
+                    lhsT=lhs_words[:, cols].bitcast(FP8X4),
+                    lhsT_scale=lhs_scales[:, cols],
+                    rhs=rhs_words[:].bitcast(FP8X4),
+                    rhs_scale=rhs_scales[:],
+                    start=True,
+                    stop=True,
+                )
+                banks.append(acc)
+            return banks
+
+        wb_words, wb_scales = quantize_weight("wb", wb_raw, (nc.scalar.copy, nc.scalar.copy))
+        b_ps = product(0, xb_words, xb_scales, wb_words, wb_scales)
+        b_rows = [sb("b_rows%d" % t, [P, H], F32) for t in range(PACK)]
+        z2_rows = sb("z2_rows", [P, PACK, H], BF16)
+        for t in range(PACK):
+            nc.scalar.activation(b_rows[t][:], b_ps[t][:], ACT.Copy, scale=gt_abs[:, t : t + 1])
+            nc.vector.tensor_scalar(
+                z2_rows[:, t, :], b_ps[t][:], gi_signed[:, t : t + 1], None, ALU.mult
+            )
+
+        wa_words, wa_scales = quantize_weight(
+            "wa", wa_raw, (nc.vector.tensor_copy, nc.vector.tensor_copy)
+        )
+        a_ps = product(PACK, xa_words, xa_scales, wa_words, wa_scales)
+        a_rows = [sb("a_rows%d" % t, [P, H], F32) for t in range(PACK)]
+
+        z2_grouped = sb("z2_grouped", [P, H, PACK], BF16)
+        interleave(nc.vector.tensor_copy, z2_grouped[:], z2_rows[:])
+
+        for t in range(PACK):
+            nc.scalar.activation(a_rows[t][:], a_ps[t][:], ACT.Copy, scale=gt_abs[:, t : t + 1])
+
+        z2_words = sb("z2_words", [P, H], U32)
+        z2_scales = sb("z2_scales", [P, H], U8)
+        quantize(z2_words[:], z2_scales[:], z2_grouped[:].rearrange("p c t -> p (c t)"))
+
+        z_words = sb("z_words", [P, H], U32)
+        z_scales = sb("z_scales", [P, H], U8)
+        for h in range(2):
+            lo, hi = h * HALF, (h + 1) * HALF
+            sums = [sb("sum%d_%d" % (i, h), [P, PACK, HALF], F32) for i in range(2)]
+            for t in range(PACK):
+                for i, (a_list, b_list) in enumerate(((n1_l, n3_l), (n2_l, n4_l))):
+                    b_picked = sb("b_picked%d_%d_%d" % (i, h, t), [P, HALF], F32)
+                    nc.scalar.activation(
+                        b_picked[:], b_rows[t][:].indirect(entries(b_list, lo, hi)), ACT.Copy
+                    )
+                    nc.vector.tensor_tensor(
+                        sums[i][:, t, :],
+                        a_rows[t][:].indirect(entries(a_list, lo, hi)),
+                        b_picked[:],
+                        ALU.add,
+                    )
+            z_grouped = sb("z_grouped%d" % h, [P, PACK, HALF // PACK, PACK], BF16)
+            nc.vector.tensor_tensor(
+                z_grouped[:].rearrange("p r m t -> p m t r"),
+                sums[0][:].rearrange("p t (m r) -> p m t r", r=PACK),
+                sums[1][:].rearrange("p t (m r) -> p m t r", r=PACK),
+                ALU.max,
+            )
+            for r in range(PACK):
+                cols = slice(r * P + lo // PACK, r * P + hi // PACK)
+                quantize(
+                    z_words[:, cols],
+                    z_scales[:, cols],
+                    z_grouped[:, r, :, :].rearrange("p m t -> p (m t)"),
+                )
+
+        cv_ps = product(0, z_words, z_scales, z2_words, z2_scales)
+        cv_rows = [sb("cv_rows%d" % r, [P, H], F32) for r in range(PACK)]
+        nc.scalar.activation(cv_rows[0][:], cv_ps[0][:], ACT.Copy, scale=CV_SCALE)
+        for r in range(1, PACK):
+            nc.vector.tensor_scalar(cv_rows[r][:], cv_ps[r][:], CV_SCALE, None, ALU.mult)
+
+        y_words = sb("y_words", [P, H], U32)
+        y_scales = sb("y_scales", [P, H], U8)
+        out_rows = out_0.rearrange("(p r) c -> p r c", r=PACK)
+        out_words = out_1[0].rearrange("p n r -> p (n r)").bitcast(I32)
+        for h in range(2):
+            lo, hi = h * HALF, (h + 1) * HALF
+            y = sb("y%d" % h, [P, PACK, HALF], F32)
+            for r in range(PACK):
+                gate = sb("gate%d_%d" % (h, r), [P, HALF], F32)
+                nc.scalar.activation(
+                    gate[:], cv_rows[r][:].indirect(entries(n5_l, lo, hi)), ACT.Sigmoid
+                )
+                nc.vector.tensor_tensor(y[:, r, :], cv_rows[r][:, lo:hi], gate[:], ALU.mult)
+            nc.sync.dma_start(out_rows[:, :, lo:hi], y[:])
+            y_grouped = sb("y_grouped%d" % h, [P, HALF, PACK], BF16)
+            interleave(nc.vector.tensor_copy, y_grouped[:], y[:])
+            quantize(
+                y_words[:, lo:hi], y_scales[:, lo:hi], y_grouped[:].rearrange("p c t -> p (c t)")
+            )
+            nc.sync.dma_start(out_words[:, lo:hi], y_words[:, lo:hi].bitcast(I32))
+        for q in range(4):
+            queue = nc.scalar if q % 2 else nc.sync
+            queue.dma_start(
+                out_2[0, 4 * q : 4 * q + 4, :].bitcast(I32),
+                y_scales[32 * q : 32 * q + 4, :].bitcast(I32),
+            )

@@ -1,7 +1,6 @@
 from contextlib import ExitStack
 
 import concourse.mybir as mybir
-from concourse.masks import make_identity
 
 K, T, S, H = 512, 2048, 512, 512
 FLOPS = 2 * K * S * H * 2 + 2 * S * H * H
@@ -20,6 +19,8 @@ P = 128
 PACK = 4
 HALF = H // 2
 CV_SCALE = 0.0625
+PLAIN_TILES = 1
+OUT_CHUNKS = ((0, 256), (256, 512))
 
 
 def tile_picked_momtpathbgate_none_po_kernel(
@@ -31,8 +32,8 @@ def tile_picked_momtpathbgate_none_po_kernel(
         keep = ctx.enter_context(tc.tile_pool(name="keep", bufs=1))
         psum = ctx.enter_context(tc.psum_pool(name="psum", bufs=1))
 
-        def sb(name, shape, dtype):
-            return keep.tile(shape, dtype, name=name, align_bytes=64)
+        def sb(name, shape, dtype, tag=None):
+            return keep.tile(shape, dtype, name=name, tag=tag or name, align_bytes=64)
 
         def bank(i):
             return psum.tile([P, H], F32, name="bank%d" % i, tag="bank%d" % i)
@@ -45,81 +46,75 @@ def tile_picked_momtpathbgate_none_po_kernel(
         def entries(lst, lo, hi):
             return lst[:, lo // 16 : hi // 16]
 
-        x_scale_table = sb("x_scale_table", [P, T], U8)
-        nc.vector.memset(x_scale_table[:].bitcast(I32), 0)
-        two_l = load_list("two_l", two)
-        offs_l = load_list("offs_l", offs)
+        x_scale_rows = sb("x_scale_rows", [P, T], U8)
         for q in range(4):
             nc.sync.dma_start(
-                x_scale_table[32 * q : 32 * q + 4, :].bitcast(I32),
+                x_scale_rows[32 * q : 32 * q + 4, :].bitcast(I32),
                 x_scales[0, 4 * q : 4 * q + 4, :].bitcast(I32),
             )
+        two_l = load_list("two_l", two)
+        offs_l = load_list("offs_l", offs)
+        wb_raw = sb("wb_raw", [P, PACK, H], F32)
+        nc.sync.dma_start(wb_raw[:], wb.rearrange("(p j) c -> p j c", j=PACK))
         x_word_table = sb("x_word_table", [P, T], U32)
         nc.sync.dma_start(
             x_word_table[:].bitcast(I32),
             x_words[0].rearrange("p n r -> p (n r)").bitcast(I32),
         )
-
-        def load_weight(name, w):
-            halves = []
-            for h in range(2):
-                raw = sb("%s_raw%d" % (name, h), [P, PACK, HALF], F32)
-                nc.sync.dma_start(
-                    raw[:], w[:, h * HALF : (h + 1) * HALF].rearrange("(p j) c -> p j c", j=PACK)
-                )
-                halves.append(raw)
-            return halves
-
-        wb_raw = load_weight("wb", wb)
-        gate_rows = sb("gate_rows", [P, P], F32)
-        nc.gpsimd.memset(gate_rows[:], 0.0)
-        ident = sb("ident", [P, P], F32)
-        make_identity(nc, ident[:])
-        for i, g in enumerate((gt, gi)):
-            nc.sync.dma_start(
-                gate_rows[PACK * i : PACK * (i + 1), :].rearrange("t (b u) -> t b u", u=8),
-                g.rearrange("(b t u) o -> t b (u o)", t=PACK, u=8),
-            )
-        wa_raw = load_weight("wa", wa)
+        gt_rows = sb("gt_rows", [P, PACK], F32)
+        gi_rows = sb("gi_rows", [P, PACK], F32)
+        nc.sync.dma_start(gt_rows[:], gt.rearrange("(p t) o -> p (t o)", t=PACK))
+        nc.sync.dma_start(gi_rows[:], gi.rearrange("(p t) o -> p (t o)", t=PACK))
         n3_l = load_list("n3_l", n3)
         n4_l = load_list("n4_l", n4)
+        wa_raw = []
+        for h in range(2):
+            raw = sb("wa_raw%d" % h, [P, PACK, HALF], F32)
+            nc.sync.dma_start(
+                raw[:], wa[:, h * HALF : (h + 1) * HALF].rearrange("(p j) c -> p j c", j=PACK)
+            )
+            wa_raw.append(raw[:])
         n1_l = load_list("n1_l", n1)
         n2_l = load_list("n2_l", n2)
         n5_l = load_list("n5_l", n5)
 
-        gate_ps = psum.tile([P, P], F32, name="gate_ps", tag="bank7")
-        nc.tensor.transpose(gate_ps[:], gate_rows[:], ident[:])
-        gt_abs = sb("gt_abs", [P, PACK], F32)
+        x_scale_table = sb("x_scale_table", [P, T], U8)
+        nc.vector.memset(x_scale_table[:].bitcast(I32), 0)
+        for q in range(4):
+            nc.vector.tensor_copy(
+                x_scale_table[32 * q : 32 * q + 4, :].bitcast(I32),
+                x_scale_rows[32 * q : 32 * q + 4, :].bitcast(I32),
+            )
+
+        warm = sb("warm", [P, 1], F32)
+        nc.scalar.activation(warm[:], wb_raw[:, 0, 0:1], ACT.Sigmoid)
+
+        gt_neg = sb("gt_neg", [P, PACK], F32)
         gt_sign = sb("gt_sign", [P, PACK], F32)
-        gi_plain = sb("gi_plain", [P, PACK], F32)
+        gt_abs = sb("gt_abs", [P, PACK], F32)
         gi_signed = sb("gi_signed", [P, PACK], F32)
-        nc.scalar.activation(gt_abs[:], gate_ps[:, 0:PACK], ACT.Abs)
-        nc.scalar.activation(gt_sign[:], gate_ps[:, 0:PACK], ACT.Sign)
-        nc.scalar.copy(gi_plain[:], gate_ps[:, PACK : 2 * PACK])
-        nc.gpsimd.tensor_tensor(gi_signed[:], gi_plain[:], gt_sign[:], ALU.mult)
+        nc.gpsimd.tensor_scalar(gt_neg[:], gt_rows[:], 0.0, -2.0, ALU.is_lt, ALU.mult)
+        nc.gpsimd.tensor_scalar(gt_sign[:], gt_neg[:], 1.0, 1.0, ALU.mult, ALU.add)
+        nc.gpsimd.tensor_tensor(gt_abs[:], gt_rows[:], gt_sign[:], ALU.mult)
+        nc.gpsimd.tensor_tensor(gi_signed[:], gi_rows[:], gt_sign[:], ALU.mult)
 
         def pick_scales(name, lst):
             picked = sb(name + "_picked", [P, S], U8)
             nc.vector.tensor_copy(picked[:], x_scale_table[:].indirect(lst[:]))
             dealt = sb(name, [P, S], U8)
             nc.vector.tensor_copy(
-                dealt[:].bitcast(I32).rearrange("p (t b w) -> p t b w", t=PACK, w=2),
-                picked[:].bitcast(I32).rearrange("p (b t w) -> p t b w", t=PACK, w=2),
+                dealt[:].rearrange("p (t m) -> p t m", t=PACK),
+                picked[:].rearrange("p (m t) -> p t m", t=PACK),
             )
             return dealt
 
         def pick_words(name, lst):
             dealt = sb(name, [P, S], U32)
             nc.vector.tensor_copy(
-                dealt[:].rearrange("p (t b u) -> p b t u", t=PACK, u=8),
+                dealt[:].rearrange("p (t m) -> p m t", t=PACK),
                 x_word_table[:].indirect(lst[:]),
             )
             return dealt
-
-        xb_scales = pick_scales("xb_scales", two_l)
-        xa_scales = pick_scales("xa_scales", offs_l)
-        xb_words = pick_words("xb_words", two_l)
-        xa_words = pick_words("xa_words", offs_l)
 
         def interleave(copy, dst, src):
             copy(
@@ -135,7 +130,7 @@ def tile_picked_momtpathbgate_none_po_kernel(
             scales = sb(name + "_scales", [P, H], U8)
             grouped = [sb("%s_grouped%d" % (name, h), [P, HALF, PACK], BF16) for h in range(2)]
             for h in range(2):
-                interleave(copies[h], grouped[h][:], raw[h][:])
+                interleave(copies[h], grouped[h][:], raw[h])
             for h in range(2):
                 cols = slice(h * HALF, (h + 1) * HALF)
                 quantize(words[:, cols], scales[:, cols], grouped[h][:].rearrange("p c t -> p (c t)"))
@@ -158,63 +153,93 @@ def tile_picked_momtpathbgate_none_po_kernel(
                 banks.append(acc)
             return banks
 
-        wb_words, wb_scales = quantize_weight("wb", wb_raw, (nc.scalar.copy, nc.scalar.copy))
+        xb_scales = pick_scales("xb_scales", two_l)
+        wb_halves = [wb_raw[:, :, h * HALF : (h + 1) * HALF] for h in range(2)]
+        wb_words, wb_scales = quantize_weight("wb", wb_halves, (nc.scalar.copy, nc.scalar.copy))
+        xa_scales = pick_scales("xa_scales", offs_l)
+        xb_words = pick_words("xb_words", two_l)
         b_ps = product(0, xb_words, xb_scales, wb_words, wb_scales)
-        b_rows = [sb("b_rows%d" % t, [P, H], F32) for t in range(PACK)]
-        z2_rows = sb("z2_rows", [P, PACK, H], BF16)
-        for t in range(PACK):
-            nc.scalar.activation(b_rows[t][:], b_ps[t][:], ACT.Copy, scale=gt_abs[:, t : t + 1])
-            nc.vector.tensor_scalar(
-                z2_rows[:, t, :], b_ps[t][:], gi_signed[:, t : t + 1], None, ALU.mult
-            )
-
+        xa_words = pick_words("xa_words", offs_l)
         wa_words, wa_scales = quantize_weight(
             "wa", wa_raw, (nc.vector.tensor_copy, nc.vector.tensor_copy)
         )
         a_ps = product(PACK, xa_words, xa_scales, wa_words, wa_scales)
+        b_rows = [sb("b_rows%d" % t, [P, H], F32) for t in range(PACK)]
         a_rows = [sb("a_rows%d" % t, [P, H], F32) for t in range(PACK)]
-
-        z2_grouped = sb("z2_grouped", [P, H, PACK], BF16)
-        interleave(nc.vector.tensor_copy, z2_grouped[:], z2_rows[:])
-
-        for t in range(PACK):
-            nc.scalar.activation(a_rows[t][:], a_ps[t][:], ACT.Copy, scale=gt_abs[:, t : t + 1])
-
         z2_words = sb("z2_words", [P, H], U32)
         z2_scales = sb("z2_scales", [P, H], U8)
-        quantize(z2_words[:], z2_scales[:], z2_grouped[:].rearrange("p c t -> p (c t)"))
-
         z_words = sb("z_words", [P, H], U32)
         z_scales = sb("z_scales", [P, H], U8)
-        for h in range(2):
-            lo, hi = h * HALF, (h + 1) * HALF
-            sums = [sb("sum%d_%d" % (i, h), [P, PACK, HALF], F32) for i in range(2)]
-            for t in range(PACK):
-                for i, (a_list, b_list) in enumerate(((n1_l, n3_l), (n2_l, n4_l))):
-                    b_picked = sb("b_picked%d_%d_%d" % (i, h, t), [P, HALF], F32)
-                    nc.scalar.activation(
-                        b_picked[:], b_rows[t][:].indirect(entries(b_list, lo, hi)), ACT.Copy
-                    )
-                    nc.vector.tensor_tensor(
-                        sums[i][:, t, :],
-                        a_rows[t][:].indirect(entries(a_list, lo, hi)),
-                        b_picked[:],
-                        ALU.add,
-                    )
-            z_grouped = sb("z_grouped%d" % h, [P, PACK, HALF // PACK, PACK], BF16)
+        sums = [[sb("sum%d_%d" % (i, h), [P, PACK, HALF], F32) for i in range(2)] for h in range(2)]
+        z_grouped = [sb("z_grouped%d" % h, [P, PACK, HALF // PACK, PACK], BF16) for h in range(2)]
+        pairs = ((n1_l, n3_l), (n2_l, n4_l))
+
+        def scaled_on_scalar(dst, src, factor):
+            nc.scalar.activation(dst, src, ACT.Copy, scale=factor)
+
+        def scaled_on_vector(dst, src, factor):
+            nc.vector.tensor_scalar(dst, src, factor, None, ALU.mult)
+
+        def fetch(name, tag, rows, lst, h):
+            picked = sb(name, [P, HALF], F32, tag=tag)
+            nc.scalar.activation(
+                picked[:], rows[:].indirect(entries(lst, h * HALF, (h + 1) * HALF)), ACT.Copy
+            )
+            return picked
+
+        def fetch_b(h, t):
+            return [
+                fetch("b_picked%d_%d_%d" % (i, h, t), "b_picked%d_%d" % (i, t), b_rows[t], pairs[i][1], h)
+                for i in range(2)
+            ]
+
+        def add_a(h, t, b_picked, fused):
+            for i in range(2):
+                if fused:
+                    a_side = a_rows[t][:].indirect(entries(pairs[i][0], h * HALF, (h + 1) * HALF))
+                else:
+                    a_side = fetch("a_picked%d_%d_%d" % (i, h, t), None, a_rows[t], pairs[i][0], h)[:]
+                nc.vector.tensor_tensor(sums[h][i][:, t, :], a_side, b_picked[i][:], ALU.add)
+
+        def larger(h):
             nc.vector.tensor_tensor(
-                z_grouped[:].rearrange("p r m t -> p m t r"),
-                sums[0][:].rearrange("p t (m r) -> p m t r", r=PACK),
-                sums[1][:].rearrange("p t (m r) -> p m t r", r=PACK),
+                z_grouped[h][:].rearrange("p r m t -> p m t r"),
+                sums[h][0][:].rearrange("p t (m r) -> p m t r", r=PACK),
+                sums[h][1][:].rearrange("p t (m r) -> p m t r", r=PACK),
                 ALU.max,
             )
+
+        def quantize_z(h):
             for r in range(PACK):
-                cols = slice(r * P + lo // PACK, r * P + hi // PACK)
+                cols = slice(r * P + h * HALF // PACK, r * P + (h + 1) * HALF // PACK)
                 quantize(
                     z_words[:, cols],
                     z_scales[:, cols],
-                    z_grouped[:, r, :, :].rearrange("p m t -> p (m t)"),
+                    z_grouped[h][:, r, :, :].rearrange("p m t -> p (m t)"),
                 )
+
+        for t in range(PACK):
+            scaled_on_scalar(b_rows[t][:], b_ps[t][:], gt_abs[:, t : t + 1])
+            b_picked = fetch_b(0, t)
+            scaled_on_vector(a_rows[t][:], a_ps[t][:], gt_abs[:, t : t + 1])
+            add_a(0, t, b_picked, True)
+        larger(0)
+        quantize_z(0)
+        for t in range(PACK):
+            add_a(1, t, fetch_b(1, t), t >= PLAIN_TILES)
+        z2_rows = sb("z2_rows", [P, PACK, H], BF16, tag="sum0_0")
+        for t in range(PACK):
+            scaled_on_scalar(z2_rows[:, t, :], b_ps[t][:], gi_signed[:, t : t + 1])
+        larger(1)
+        z2_grouped = [sb("z2_grouped%d" % h, [P, HALF, PACK], BF16) for h in range(2)]
+        for h in range(2):
+            interleave(nc.scalar.copy, z2_grouped[h][:], z2_rows[:, :, h * HALF : (h + 1) * HALF])
+        quantize_z(1)
+        for h in range(2):
+            cols = slice(h * HALF, (h + 1) * HALF)
+            quantize(
+                z2_words[:, cols], z2_scales[:, cols], z2_grouped[h][:].rearrange("p c t -> p (c t)")
+            )
 
         cv_ps = product(0, z_words, z_scales, z2_words, z2_scales)
         cv_rows = [sb("cv_rows%d" % r, [P, H], F32) for r in range(PACK)]
@@ -226,17 +251,16 @@ def tile_picked_momtpathbgate_none_po_kernel(
         y_scales = sb("y_scales", [P, H], U8)
         out_rows = out_0.rearrange("(p r) c -> p r c", r=PACK)
         out_words = out_1[0].rearrange("p n r -> p (n r)").bitcast(I32)
-        for h in range(2):
-            lo, hi = h * HALF, (h + 1) * HALF
-            y = sb("y%d" % h, [P, PACK, HALF], F32)
+        for h, (lo, hi) in enumerate(OUT_CHUNKS):
+            y = sb("y%d" % h, [P, PACK, hi - lo], F32)
             for r in range(PACK):
-                gate = sb("gate%d_%d" % (h, r), [P, HALF], F32)
+                gate = sb("gate%d_%d" % (h, r), [P, hi - lo], F32)
                 nc.scalar.activation(
                     gate[:], cv_rows[r][:].indirect(entries(n5_l, lo, hi)), ACT.Sigmoid
                 )
                 nc.vector.tensor_tensor(y[:, r, :], cv_rows[r][:, lo:hi], gate[:], ALU.mult)
             nc.sync.dma_start(out_rows[:, :, lo:hi], y[:])
-            y_grouped = sb("y_grouped%d" % h, [P, HALF, PACK], BF16)
+            y_grouped = sb("y_grouped%d" % h, [P, hi - lo, PACK], BF16)
             interleave(nc.vector.tensor_copy, y_grouped[:], y[:])
             quantize(
                 y_words[:, lo:hi], y_scales[:, lo:hi], y_grouped[:].rearrange("p c t -> p (c t)")

@@ -19,7 +19,7 @@ P = 128
 PACK = 4
 HALF = H // 2
 CV_SCALE = 0.0625
-PLAIN_TILES = 1
+PLAIN_TILES = 2
 OUT_CHUNKS = ((0, 256), (256, 512))
 
 
@@ -56,24 +56,19 @@ def tile_picked_momtpathbgate_none_po_kernel(
         offs_l = load_list("offs_l", offs)
         wb_raw = sb("wb_raw", [P, PACK, H], F32)
         nc.sync.dma_start(wb_raw[:], wb.rearrange("(p j) c -> p j c", j=PACK))
-        x_word_table = sb("x_word_table", [P, T], U32)
-        nc.sync.dma_start(
-            x_word_table[:].bitcast(I32),
-            x_words[0].rearrange("p n r -> p (n r)").bitcast(I32),
-        )
+        wa_raw = sb("wa_raw", [P, PACK, H], F32)
+        nc.sync.dma_start(wa_raw[:], wa.rearrange("(p j) c -> p j c", j=PACK))
         gt_rows = sb("gt_rows", [P, PACK], F32)
         gi_rows = sb("gi_rows", [P, PACK], F32)
         nc.sync.dma_start(gt_rows[:], gt.rearrange("(p t) o -> p (t o)", t=PACK))
         nc.sync.dma_start(gi_rows[:], gi.rearrange("(p t) o -> p (t o)", t=PACK))
         n3_l = load_list("n3_l", n3)
         n4_l = load_list("n4_l", n4)
-        wa_raw = []
-        for h in range(2):
-            raw = sb("wa_raw%d" % h, [P, PACK, HALF], F32)
-            nc.sync.dma_start(
-                raw[:], wa[:, h * HALF : (h + 1) * HALF].rearrange("(p j) c -> p j c", j=PACK)
-            )
-            wa_raw.append(raw[:])
+        x_word_table = sb("x_word_table", [P, T], U32)
+        nc.sync.dma_start(
+            x_word_table[:].bitcast(I32),
+            x_words[0].rearrange("p n r -> p (n r)").bitcast(I32),
+        )
         n1_l = load_list("n1_l", n1)
         n2_l = load_list("n2_l", n2)
         n5_l = load_list("n5_l", n5)
@@ -130,40 +125,35 @@ def tile_picked_momtpathbgate_none_po_kernel(
             scales = sb(name + "_scales", [P, H], U8)
             grouped = [sb("%s_grouped%d" % (name, h), [P, HALF, PACK], BF16) for h in range(2)]
             for h in range(2):
-                interleave(copies[h], grouped[h][:], raw[h])
+                interleave(copies[h], grouped[h][:], raw[:, :, h * HALF : (h + 1) * HALF])
             for h in range(2):
                 cols = slice(h * HALF, (h + 1) * HALF)
                 quantize(words[:, cols], scales[:, cols], grouped[h][:].rearrange("p c t -> p (c t)"))
             return words, scales
 
-        def product(first_bank, lhs_words, lhs_scales, rhs_words, rhs_scales):
-            banks = []
-            for t in range(PACK):
-                acc = bank(first_bank + t)
-                cols = slice(t * P, (t + 1) * P)
-                nc.tensor.matmul_mx(
-                    out=acc[:],
-                    lhsT=lhs_words[:, cols].bitcast(FP8X4),
-                    lhsT_scale=lhs_scales[:, cols],
-                    rhs=rhs_words[:].bitcast(FP8X4),
-                    rhs_scale=rhs_scales[:],
-                    start=True,
-                    stop=True,
-                )
-                banks.append(acc)
-            return banks
+        def product(t, acc, lhs_words, lhs_scales, rhs_words, rhs_scales):
+            cols = slice(t * P, (t + 1) * P)
+            nc.tensor.matmul_mx(
+                out=acc[:],
+                lhsT=lhs_words[:, cols].bitcast(FP8X4),
+                lhsT_scale=lhs_scales[:, cols],
+                rhs=rhs_words[:].bitcast(FP8X4),
+                rhs_scale=rhs_scales[:],
+                start=True,
+                stop=True,
+            )
 
         xb_scales = pick_scales("xb_scales", two_l)
-        wb_halves = [wb_raw[:, :, h * HALF : (h + 1) * HALF] for h in range(2)]
-        wb_words, wb_scales = quantize_weight("wb", wb_halves, (nc.scalar.copy, nc.scalar.copy))
+        wb_words, wb_scales = quantize_weight("wb", wb_raw, (nc.scalar.copy, nc.scalar.copy))
         xa_scales = pick_scales("xa_scales", offs_l)
+        wa_words, wa_scales = quantize_weight("wa", wa_raw, (nc.vector.tensor_copy, nc.scalar.copy))
         xb_words = pick_words("xb_words", two_l)
-        b_ps = product(0, xb_words, xb_scales, wb_words, wb_scales)
         xa_words = pick_words("xa_words", offs_l)
-        wa_words, wa_scales = quantize_weight(
-            "wa", wa_raw, (nc.vector.tensor_copy, nc.vector.tensor_copy)
-        )
-        a_ps = product(PACK, xa_words, xa_scales, wa_words, wa_scales)
+        b_ps = [bank(t) for t in range(PACK)]
+        a_ps = [bank(PACK + t) for t in range(PACK)]
+        for t in range(PACK):
+            product(t, b_ps[t], xb_words, xb_scales, wb_words, wb_scales)
+            product(t, a_ps[t], xa_words, xa_scales, wa_words, wa_scales)
         b_rows = [sb("b_rows%d" % t, [P, H], F32) for t in range(PACK)]
         a_rows = [sb("a_rows%d" % t, [P, H], F32) for t in range(PACK)]
         z2_words = sb("z2_words", [P, H], U32)
@@ -198,7 +188,8 @@ def tile_picked_momtpathbgate_none_po_kernel(
                 if fused:
                     a_side = a_rows[t][:].indirect(entries(pairs[i][0], h * HALF, (h + 1) * HALF))
                 else:
-                    a_side = fetch("a_picked%d_%d_%d" % (i, h, t), None, a_rows[t], pairs[i][0], h)[:]
+                    tag = "b_picked%d_%d" % (i, PACK - 1 - t)
+                    a_side = fetch("a_picked%d_%d" % (i, t), tag, a_rows[t], pairs[i][0], h)[:]
                 nc.vector.tensor_tensor(sums[h][i][:, t, :], a_side, b_picked[i][:], ALU.add)
 
         def larger(h):
@@ -232,8 +223,8 @@ def tile_picked_momtpathbgate_none_po_kernel(
             scaled_on_scalar(z2_rows[:, t, :], b_ps[t][:], gi_signed[:, t : t + 1])
         larger(1)
         z2_grouped = [sb("z2_grouped%d" % h, [P, HALF, PACK], BF16) for h in range(2)]
-        for h in range(2):
-            interleave(nc.scalar.copy, z2_grouped[h][:], z2_rows[:, :, h * HALF : (h + 1) * HALF])
+        for h, copy in enumerate((nc.vector.tensor_copy, nc.scalar.copy)):
+            interleave(copy, z2_grouped[h][:], z2_rows[:, :, h * HALF : (h + 1) * HALF])
         quantize_z(1)
         for h in range(2):
             cols = slice(h * HALF, (h + 1) * HALF)
@@ -241,20 +232,21 @@ def tile_picked_momtpathbgate_none_po_kernel(
                 z2_words[:, cols], z2_scales[:, cols], z2_grouped[h][:].rearrange("p c t -> p (c t)")
             )
 
-        cv_ps = product(0, z_words, z_scales, z2_words, z2_scales)
+        cv_ps = [bank(PACK + r) for r in range(PACK)]
+        for r in range(PACK):
+            product(r, cv_ps[r], z_words, z_scales, z2_words, z2_scales)
         cv_rows = [sb("cv_rows%d" % r, [P, H], F32) for r in range(PACK)]
         nc.scalar.activation(cv_rows[0][:], cv_ps[0][:], ACT.Copy, scale=CV_SCALE)
         for r in range(1, PACK):
             nc.vector.tensor_scalar(cv_rows[r][:], cv_ps[r][:], CV_SCALE, None, ALU.mult)
 
-        y_words = sb("y_words", [P, H], U32)
         y_scales = sb("y_scales", [P, H], U8)
         out_rows = out_0.rearrange("(p r) c -> p r c", r=PACK)
         out_words = out_1[0].rearrange("p n r -> p (n r)").bitcast(I32)
         for h, (lo, hi) in enumerate(OUT_CHUNKS):
             y = sb("y%d" % h, [P, PACK, hi - lo], F32)
             for r in range(PACK):
-                gate = sb("gate%d_%d" % (h, r), [P, hi - lo], F32)
+                gate = sb("gate%d_%d" % (h, r), [P, hi - lo], F32, tag="gate%d" % r)
                 nc.scalar.activation(
                     gate[:], cv_rows[r][:].indirect(entries(n5_l, lo, hi)), ACT.Sigmoid
                 )
@@ -262,10 +254,9 @@ def tile_picked_momtpathbgate_none_po_kernel(
             nc.sync.dma_start(out_rows[:, :, lo:hi], y[:])
             y_grouped = sb("y_grouped%d" % h, [P, hi - lo, PACK], BF16)
             interleave(nc.vector.tensor_copy, y_grouped[:], y[:])
-            quantize(
-                y_words[:, lo:hi], y_scales[:, lo:hi], y_grouped[:].rearrange("p c t -> p (c t)")
-            )
-            nc.sync.dma_start(out_words[:, lo:hi], y_words[:, lo:hi].bitcast(I32))
+            y_words = sb("y_words%d" % h, [P, hi - lo], U32)
+            quantize(y_words[:], y_scales[:, lo:hi], y_grouped[:].rearrange("p c t -> p (c t)"))
+            nc.sync.dma_start(out_words[:, lo:hi], y_words[:].bitcast(I32))
         for q in range(4):
             queue = nc.scalar if q % 2 else nc.sync
             queue.dma_start(

@@ -19,7 +19,6 @@ P = 128
 PACK = 4
 HALF = H // 2
 CV_SCALE = 0.0625
-PLAIN_TILES = 2
 OUT_CHUNKS = ((0, 256), (256, 512))
 
 
@@ -75,6 +74,10 @@ def tile_picked_momtpathbgate_none_po_kernel(
 
         x_scale_table = sb("x_scale_table", [P, T], U8)
         nc.vector.memset(x_scale_table[:].bitcast(I32), 0)
+        b_rows = [sb("b_rows%d" % t, [P, 2 * H], F32) for t in range(PACK)]
+        a_rows = [sb("a_rows%d" % t, [P, 2 * H], F32) for t in range(PACK)]
+        for rows in (b_rows[0], a_rows[0]):
+            nc.vector.memset(rows[:, H : 2 * H], 0.0)
         for q in range(4):
             nc.vector.tensor_copy(
                 x_scale_table[32 * q : 32 * q + 4, :].bitcast(I32),
@@ -151,81 +154,59 @@ def tile_picked_momtpathbgate_none_po_kernel(
         xa_words = pick_words("xa_words", offs_l)
         b_ps = [bank(t) for t in range(PACK)]
         a_ps = [bank(PACK + t) for t in range(PACK)]
+        product(0, b_ps[0], xb_words, xb_scales, wb_words, wb_scales)
         for t in range(PACK):
-            product(t, b_ps[t], xb_words, xb_scales, wb_words, wb_scales)
             product(t, a_ps[t], xa_words, xa_scales, wa_words, wa_scales)
-        b_rows = [sb("b_rows%d" % t, [P, H], F32) for t in range(PACK)]
-        a_rows = [sb("a_rows%d" % t, [P, H], F32) for t in range(PACK)]
-        z2_words = sb("z2_words", [P, H], U32)
-        z2_scales = sb("z2_scales", [P, H], U8)
-        z_words = sb("z_words", [P, H], U32)
-        z_scales = sb("z_scales", [P, H], U8)
-        sums = [[sb("sum%d_%d" % (i, h), [P, PACK, HALF], F32) for i in range(2)] for h in range(2)]
-        z_grouped = [sb("z_grouped%d" % h, [P, PACK, HALF // PACK, PACK], BF16) for h in range(2)]
-        pairs = ((n1_l, n3_l), (n2_l, n4_l))
+        for t in range(1, PACK):
+            product(t, b_ps[t], xb_words, xb_scales, wb_words, wb_scales)
 
         def scaled_on_scalar(dst, src, factor):
             nc.scalar.activation(dst, src, ACT.Copy, scale=factor)
 
-        def scaled_on_vector(dst, src, factor):
-            nc.vector.tensor_scalar(dst, src, factor, None, ALU.mult)
+        def fetch(picked, rows, lst):
+            nc.scalar.activation(picked, rows[:].indirect(lst[:]), ACT.Copy)
 
-        def fetch(name, tag, rows, lst, h):
-            picked = sb(name, [P, HALF], F32, tag=tag)
-            nc.scalar.activation(
-                picked[:], rows[:].indirect(entries(lst, h * HALF, (h + 1) * HALF)), ACT.Copy
+        last_b_picked = sb("last_b_picked", [P, 2, H], F32)
+        a_picked = sb("a_picked", [P, 2, H], F32)
+        sums = [sb("sum%d" % i, [P, PACK, H], F32) for i in range(2)]
+        for t in range(PACK):
+            last = t == PACK - 1
+            if last:
+                b_picked = (last_b_picked[:, 0, :], last_b_picked[:, 1, :])
+            else:
+                b_picked = (a_rows[t + 1][:, H : 2 * H], b_rows[t + 1][:, H : 2 * H])
+            scaled_on_scalar(b_rows[t][:, 0:H], b_ps[t][:], gt_abs[:, t : t + 1])
+            for i, lst in enumerate((n3_l, n4_l)):
+                fetch(b_picked[i], b_rows[t], lst)
+            nc.vector.tensor_scalar(
+                a_rows[t][:, 0:H], a_ps[t][:], gt_abs[:, t : t + 1], None, ALU.mult
             )
-            return picked
-
-        def fetch_b(h, t):
-            return [
-                fetch("b_picked%d_%d_%d" % (i, h, t), "b_picked%d_%d" % (i, t), b_rows[t], pairs[i][1], h)
-                for i in range(2)
-            ]
-
-        def add_a(h, t, b_picked, fused):
-            for i in range(2):
-                if fused:
-                    a_side = a_rows[t][:].indirect(entries(pairs[i][0], h * HALF, (h + 1) * HALF))
+            for i, lst in enumerate((n1_l, n2_l)):
+                if last:
+                    fetch(a_picked[:, i, :], a_rows[t], lst)
+                    a_side = a_picked[:, i, :]
                 else:
-                    tag = "b_picked%d_%d" % (i, PACK - 1 - t)
-                    a_side = fetch("a_picked%d_%d" % (i, t), tag, a_rows[t], pairs[i][0], h)[:]
-                nc.vector.tensor_tensor(sums[h][i][:, t, :], a_side, b_picked[i][:], ALU.add)
+                    a_side = a_rows[t][:].indirect(lst[:])
+                nc.vector.tensor_tensor(sums[i][:, t, :], a_side, b_picked[i], ALU.add)
 
-        def larger(h):
-            nc.vector.tensor_tensor(
-                z_grouped[h][:].rearrange("p r m t -> p m t r"),
-                sums[h][0][:].rearrange("p t (m r) -> p m t r", r=PACK),
-                sums[h][1][:].rearrange("p t (m r) -> p m t r", r=PACK),
-                ALU.max,
-            )
-
-        def quantize_z(h):
-            for r in range(PACK):
-                cols = slice(r * P + h * HALF // PACK, r * P + (h + 1) * HALF // PACK)
-                quantize(
-                    z_words[:, cols],
-                    z_scales[:, cols],
-                    z_grouped[h][:, r, :, :].rearrange("p m t -> p (m t)"),
-                )
-
-        for t in range(PACK):
-            scaled_on_scalar(b_rows[t][:], b_ps[t][:], gt_abs[:, t : t + 1])
-            b_picked = fetch_b(0, t)
-            scaled_on_vector(a_rows[t][:], a_ps[t][:], gt_abs[:, t : t + 1])
-            add_a(0, t, b_picked, True)
-        larger(0)
-        quantize_z(0)
-        for t in range(PACK):
-            add_a(1, t, fetch_b(1, t), t >= PLAIN_TILES)
-        z2_rows = sb("z2_rows", [P, PACK, H], BF16, tag="sum0_0")
+        z2_rows = sb("z2_rows", [P, PACK, H], BF16, tag="b_rows%d" % (PACK - 1))
         for t in range(PACK):
             scaled_on_scalar(z2_rows[:, t, :], b_ps[t][:], gi_signed[:, t : t + 1])
-        larger(1)
+        z_grouped = sb("z_grouped", [P, PACK, P, PACK], BF16)
+        nc.vector.tensor_tensor(
+            z_grouped[:].rearrange("p r m t -> p m t r"),
+            sums[0][:].rearrange("p t (m r) -> p m t r", r=PACK),
+            sums[1][:].rearrange("p t (m r) -> p m t r", r=PACK),
+            ALU.max,
+        )
         z2_grouped = [sb("z2_grouped%d" % h, [P, HALF, PACK], BF16) for h in range(2)]
-        for h, copy in enumerate((nc.vector.tensor_copy, nc.scalar.copy)):
-            interleave(copy, z2_grouped[h][:], z2_rows[:, :, h * HALF : (h + 1) * HALF])
-        quantize_z(1)
+        for h in range(2):
+            interleave(nc.scalar.copy, z2_grouped[h][:], z2_rows[:, :, h * HALF : (h + 1) * HALF])
+        z_words = sb("z_words", [P, H], U32)
+        z_scales = sb("z_scales", [P, H], U8)
+        quantize(z_words[:], z_scales[:], z_grouped[:].rearrange("p r m t -> p (r m t)"))
+        z2_words = sb("z2_words", [P, H], U32)
+        z2_scales = sb("z2_scales", [P, H], U8)
         for h in range(2):
             cols = slice(h * HALF, (h + 1) * HALF)
             quantize(

@@ -18,8 +18,9 @@ ALU = mybir.AluOpType
 P = 128
 PACK = 4
 HALF = H // 2
+QUADRANT = 32
+LINE = 4
 CV_SCALE = 0.0625
-OUT_CHUNKS = ((0, 256), (256, 512))
 
 
 def tile_picked_momtpathbgate_none_po_kernel(
@@ -38,9 +39,9 @@ def tile_picked_momtpathbgate_none_po_kernel(
             return psum.tile([P, H], F32, name="bank%d" % i, tag="bank%d" % i)
 
         def load_list(name, src):
-            t = lists.tile([P, S // 16], U16, name=name)
-            nc.sync.dma_start(t[:], src)
-            return t
+            offsets = lists.tile([P, S // 16], U16, name=name)
+            nc.sync.dma_start(offsets[:], src)
+            return offsets
 
         def entries(lst, lo, hi):
             return lst[:, lo // 16 : hi // 16]
@@ -48,7 +49,7 @@ def tile_picked_momtpathbgate_none_po_kernel(
         x_scale_rows = sb("x_scale_rows", [P, T], U8)
         for q in range(4):
             nc.sync.dma_start(
-                x_scale_rows[32 * q : 32 * q + 4, :].bitcast(I32),
+                x_scale_rows[QUADRANT * q : QUADRANT * q + 4, :].bitcast(I32),
                 x_scales[0, 4 * q : 4 * q + 4, :].bitcast(I32),
             )
         two_l = load_list("two_l", two)
@@ -80,8 +81,8 @@ def tile_picked_momtpathbgate_none_po_kernel(
             nc.vector.memset(rows[:, H : 2 * H], 0.0)
         for q in range(4):
             nc.vector.tensor_copy(
-                x_scale_table[32 * q : 32 * q + 4, :].bitcast(I32),
-                x_scale_rows[32 * q : 32 * q + 4, :].bitcast(I32),
+                x_scale_table[QUADRANT * q : QUADRANT * q + 4, :].bitcast(I32),
+                x_scale_rows[QUADRANT * q : QUADRANT * q + 4, :].bitcast(I32),
             )
 
         warm = sb("warm", [P, 1], F32)
@@ -116,8 +117,8 @@ def tile_picked_momtpathbgate_none_po_kernel(
 
         def interleave(copy, dst, src):
             copy(
-                dst.rearrange("p (c i) t -> p c t i", i=4),
-                src.rearrange("p t (c i) -> p c t i", i=4),
+                dst.rearrange("p (c i) t -> p c t i", i=LINE),
+                src.rearrange("p t (c i) -> p c t i", i=LINE),
             )
 
         def quantize(words, scales, grouped):
@@ -167,7 +168,7 @@ def tile_picked_momtpathbgate_none_po_kernel(
             nc.scalar.activation(picked, rows[:].indirect(lst[:]), ACT.Copy)
 
         last_b_picked = sb("last_b_picked", [P, 2, H], F32)
-        a_picked = sb("a_picked", [P, 2, H], F32)
+        a_picked = sb("a_picked", [P, H], F32)
         sums = [sb("sum%d" % i, [P, PACK, H], F32) for i in range(2)]
         for t in range(PACK):
             last = t == PACK - 1
@@ -182,15 +183,16 @@ def tile_picked_momtpathbgate_none_po_kernel(
                 a_rows[t][:, 0:H], a_ps[t][:], gt_abs[:, t : t + 1], None, ALU.mult
             )
             for i, lst in enumerate((n1_l, n2_l)):
-                if last:
-                    fetch(a_picked[:, i, :], a_rows[t], lst)
-                    a_side = a_picked[:, i, :]
+                if last and i == 1:
+                    fetch(a_picked[:], a_rows[t], lst)
+                    a_side = a_picked[:]
                 else:
                     a_side = a_rows[t][:].indirect(lst[:])
                 nc.vector.tensor_tensor(sums[i][:, t, :], a_side, b_picked[i], ALU.add)
 
         z2_rows = sb("z2_rows", [P, PACK, H], BF16, tag="b_rows%d" % (PACK - 1))
-        for t in range(PACK):
+        nc.vector.tensor_scalar(z2_rows[:, 0, :], b_ps[0][:], gi_signed[:, 0:1], None, ALU.mult)
+        for t in range(1, PACK):
             scaled_on_scalar(z2_rows[:, t, :], b_ps[t][:], gi_signed[:, t : t + 1])
         z_grouped = sb("z_grouped", [P, PACK, P, PACK], BF16)
         nc.vector.tensor_tensor(
@@ -224,23 +226,36 @@ def tile_picked_momtpathbgate_none_po_kernel(
         y_scales = sb("y_scales", [P, H], U8)
         out_rows = out_0.rearrange("(p r) c -> p r c", r=PACK)
         out_words = out_1[0].rearrange("p n r -> p (n r)").bitcast(I32)
-        for h, (lo, hi) in enumerate(OUT_CHUNKS):
-            y = sb("y%d" % h, [P, PACK, hi - lo], F32)
+        for h in range(2):
+            lo, hi = h * HALF, (h + 1) * HALF
+            y = sb("y%d" % h, [P, PACK, HALF], F32)
             for r in range(PACK):
-                gate = sb("gate%d_%d" % (h, r), [P, hi - lo], F32, tag="gate%d" % r)
+                gate = sb("gate%d_%d" % (h, r), [P, HALF], F32, tag="gate%d" % r)
                 nc.scalar.activation(
                     gate[:], cv_rows[r][:].indirect(entries(n5_l, lo, hi)), ACT.Sigmoid
                 )
                 nc.vector.tensor_tensor(y[:, r, :], cv_rows[r][:, lo:hi], gate[:], ALU.mult)
             nc.sync.dma_start(out_rows[:, :, lo:hi], y[:])
-            y_grouped = sb("y_grouped%d" % h, [P, hi - lo, PACK], BF16)
-            interleave(nc.vector.tensor_copy, y_grouped[:], y[:])
-            y_words = sb("y_words%d" % h, [P, hi - lo], U32)
-            quantize(y_words[:], y_scales[:, lo:hi], y_grouped[:].rearrange("p c t -> p (c t)"))
+            y_words = sb("y_words%d" % h, [P, HALF], U32)
+            if h == 0:
+                shares = ((0, HALF, nc.vector.tensor_copy),)
+            else:
+                shares = ((0, HALF // 2, nc.vector.tensor_copy), (HALF // 2, HALF, nc.scalar.copy))
+            grouped = []
+            for c0, c1, copy in shares:
+                y_grouped = sb("y_grouped%d_%d" % (h, c0), [P, c1 - c0, PACK], BF16)
+                interleave(copy, y_grouped[:], y[:, :, c0:c1])
+                grouped.append(y_grouped)
+            for (c0, c1, copy), y_grouped in zip(shares, grouped):
+                quantize(
+                    y_words[:, c0:c1],
+                    y_scales[:, lo + c0 : lo + c1],
+                    y_grouped[:].rearrange("p c t -> p (c t)"),
+                )
             nc.sync.dma_start(out_words[:, lo:hi], y_words[:].bitcast(I32))
         for q in range(4):
             queue = nc.scalar if q % 2 else nc.sync
             queue.dma_start(
                 out_2[0, 4 * q : 4 * q + 4, :].bitcast(I32),
-                y_scales[32 * q : 32 * q + 4, :].bitcast(I32),
+                y_scales[QUADRANT * q : QUADRANT * q + 4, :].bitcast(I32),
             )

from contextlib import ExitStack

import concourse.mybir as mybir

K, T, S, H = 512, 2048, 512, 512
FLOPS = 2 * K * S * H * 2 + 2 * S * H * H

F32 = mybir.dt.float32
BF16 = mybir.dt.bfloat16
I32 = mybir.dt.int32
U32 = mybir.dt.uint32
U16 = mybir.dt.uint16
U8 = mybir.dt.uint8
FP8X4 = mybir.dt.float8_e4m3fn_x4
ACT = mybir.ActivationFunctionType
ALU = mybir.AluOpType

P = 128
PACK = 4
HALF = H // 2
QUADRANT = 32
LINE = 4
CV_SCALE = 0.0625


def tile_picked_momtpathbgate_none_po_kernel(
    tc, x_words, x_scales, wa, wb, gt, gi, offs, two, n1, n2, n3, n4, n5, out_0, out_1, out_2
):
    nc = tc.nc
    with ExitStack() as ctx:
        lists = ctx.enter_context(tc.tile_pool(name="lists", bufs=1))
        keep = ctx.enter_context(tc.tile_pool(name="keep", bufs=1))
        psum = ctx.enter_context(tc.psum_pool(name="psum", bufs=1))

        def sb(name, shape, dtype, tag=None):
            return keep.tile(shape, dtype, name=name, tag=tag or name, align_bytes=64)

        def bank(i):
            return psum.tile([P, H], F32, name="bank%d" % i, tag="bank%d" % i)

        def load_list(name, src):
            offsets = lists.tile([P, S // 16], U16, name=name)
            nc.sync.dma_start(offsets[:], src)
            return offsets

        def entries(lst, lo, hi):
            return lst[:, lo // 16 : hi // 16]

        x_scale_rows = sb("x_scale_rows", [P, T], U8)
        for q in range(4):
            nc.sync.dma_start(
                x_scale_rows[QUADRANT * q : QUADRANT * q + 4, :].bitcast(I32),
                x_scales[0, 4 * q : 4 * q + 4, :].bitcast(I32),
            )
        two_l = load_list("two_l", two)
        offs_l = load_list("offs_l", offs)
        wb_raw = sb("wb_raw", [P, PACK, H], F32)
        nc.sync.dma_start(wb_raw[:], wb.rearrange("(p j) c -> p j c", j=PACK))
        wa_raw = sb("wa_raw", [P, PACK, H], F32)
        nc.sync.dma_start(wa_raw[:], wa.rearrange("(p j) c -> p j c", j=PACK))
        gt_rows = sb("gt_rows", [P, PACK], F32)
        gi_rows = sb("gi_rows", [P, PACK], F32)
        nc.sync.dma_start(gt_rows[:], gt.rearrange("(p t) o -> p (t o)", t=PACK))
        nc.sync.dma_start(gi_rows[:], gi.rearrange("(p t) o -> p (t o)", t=PACK))
        n3_l = load_list("n3_l", n3)
        n4_l = load_list("n4_l", n4)
        x_word_table = sb("x_word_table", [P, T], U32)
        nc.sync.dma_start(
            x_word_table[:].bitcast(I32),
            x_words[0].rearrange("p n r -> p (n r)").bitcast(I32),
        )
        n1_l = load_list("n1_l", n1)
        n2_l = load_list("n2_l", n2)
        n5_l = load_list("n5_l", n5)

        x_scale_table = sb("x_scale_table", [P, T], U8)
        nc.vector.memset(x_scale_table[:].bitcast(I32), 0)
        b_rows = [sb("b_rows%d" % t, [P, 2 * H], F32) for t in range(PACK)]
        a_rows = [sb("a_rows%d" % t, [P, 2 * H], F32) for t in range(PACK)]
        for rows in (b_rows[0], a_rows[0]):
            nc.vector.memset(rows[:, H : 2 * H], 0.0)
        for q in range(4):
            nc.vector.tensor_copy(
                x_scale_table[QUADRANT * q : QUADRANT * q + 4, :].bitcast(I32),
                x_scale_rows[QUADRANT * q : QUADRANT * q + 4, :].bitcast(I32),
            )

        warm = sb("warm", [P, 1], F32)
        nc.scalar.activation(warm[:], wb_raw[:, 0, 0:1], ACT.Sigmoid)

        gt_neg = sb("gt_neg", [P, PACK], F32)
        gt_sign = sb("gt_sign", [P, PACK], F32)
        gt_abs = sb("gt_abs", [P, PACK], F32)
        gi_signed = sb("gi_signed", [P, PACK], F32)
        nc.gpsimd.tensor_scalar(gt_neg[:], gt_rows[:], 0.0, -2.0, ALU.is_lt, ALU.mult)
        nc.gpsimd.tensor_scalar(gt_sign[:], gt_neg[:], 1.0, 1.0, ALU.mult, ALU.add)
        nc.gpsimd.tensor_tensor(gt_abs[:], gt_rows[:], gt_sign[:], ALU.mult)
        nc.gpsimd.tensor_tensor(gi_signed[:], gi_rows[:], gt_sign[:], ALU.mult)

        def pick_scales(name, lst):
            picked = sb(name + "_picked", [P, S], U8)
            nc.vector.tensor_copy(picked[:], x_scale_table[:].indirect(lst[:]))
            dealt = sb(name, [P, S], U8)
            nc.vector.tensor_copy(
                dealt[:].rearrange("p (t m) -> p t m", t=PACK),
                picked[:].rearrange("p (m t) -> p t m", t=PACK),
            )
            return dealt

        def pick_words(name, lst):
            dealt = sb(name, [P, S], U32)
            nc.vector.tensor_copy(
                dealt[:].rearrange("p (t m) -> p m t", t=PACK),
                x_word_table[:].indirect(lst[:]),
            )
            return dealt

        def interleave(copy, dst, src):
            copy(
                dst.rearrange("p (c i) t -> p c t i", i=LINE),
                src.rearrange("p t (c i) -> p c t i", i=LINE),
            )

        def quantize(words, scales, grouped):
            nc.vector.quantize_mx(out=words.bitcast(FP8X4), scales=scales, in_=grouped)

        def quantize_weight(name, raw, copies):
            words = sb(name + "_words", [P, H], U32)
            scales = sb(name + "_scales", [P, H], U8)
            grouped = [sb("%s_grouped%d" % (name, h), [P, HALF, PACK], BF16) for h in range(2)]
            for h in range(2):
                interleave(copies[h], grouped[h][:], raw[:, :, h * HALF : (h + 1) * HALF])
            for h in range(2):
                cols = slice(h * HALF, (h + 1) * HALF)
                quantize(words[:, cols], scales[:, cols], grouped[h][:].rearrange("p c t -> p (c t)"))
            return words, scales

        def product(t, acc, lhs_words, lhs_scales, rhs_words, rhs_scales):
            cols = slice(t * P, (t + 1) * P)
            nc.tensor.matmul_mx(
                out=acc[:],
                lhsT=lhs_words[:, cols].bitcast(FP8X4),
                lhsT_scale=lhs_scales[:, cols],
                rhs=rhs_words[:].bitcast(FP8X4),
                rhs_scale=rhs_scales[:],
                start=True,
                stop=True,
            )

        xb_scales = pick_scales("xb_scales", two_l)
        wb_words, wb_scales = quantize_weight("wb", wb_raw, (nc.scalar.copy, nc.scalar.copy))
        xa_scales = pick_scales("xa_scales", offs_l)
        wa_words, wa_scales = quantize_weight("wa", wa_raw, (nc.vector.tensor_copy, nc.scalar.copy))
        xb_words = pick_words("xb_words", two_l)
        xa_words = pick_words("xa_words", offs_l)
        b_ps = [bank(t) for t in range(PACK)]
        a_ps = [bank(PACK + t) for t in range(PACK)]
        product(0, b_ps[0], xb_words, xb_scales, wb_words, wb_scales)
        for t in range(PACK):
            product(t, a_ps[t], xa_words, xa_scales, wa_words, wa_scales)
        for t in range(1, PACK):
            product(t, b_ps[t], xb_words, xb_scales, wb_words, wb_scales)

        def scaled_on_scalar(dst, src, factor):
            nc.scalar.activation(dst, src, ACT.Copy, scale=factor)

        def fetch(picked, rows, lst):
            nc.scalar.activation(picked, rows[:].indirect(lst[:]), ACT.Copy)

        last_b_picked = sb("last_b_picked", [P, 2, H], F32)
        a_picked = sb("a_picked", [P, H], F32)
        sums = [sb("sum%d" % i, [P, PACK, H], F32) for i in range(2)]
        for t in range(PACK):
            last = t == PACK - 1
            if last:
                b_picked = (last_b_picked[:, 0, :], last_b_picked[:, 1, :])
            else:
                b_picked = (a_rows[t + 1][:, H : 2 * H], b_rows[t + 1][:, H : 2 * H])
            scaled_on_scalar(b_rows[t][:, 0:H], b_ps[t][:], gt_abs[:, t : t + 1])
            for i, lst in enumerate((n3_l, n4_l)):
                fetch(b_picked[i], b_rows[t], lst)
            nc.vector.tensor_scalar(
                a_rows[t][:, 0:H], a_ps[t][:], gt_abs[:, t : t + 1], None, ALU.mult
            )
            for i, lst in enumerate((n1_l, n2_l)):
                if last and i == 1:
                    fetch(a_picked[:], a_rows[t], lst)
                    a_side = a_picked[:]
                else:
                    a_side = a_rows[t][:].indirect(lst[:])
                nc.vector.tensor_tensor(sums[i][:, t, :], a_side, b_picked[i], ALU.add)

        z2_rows = sb("z2_rows", [P, PACK, H], BF16, tag="b_rows%d" % (PACK - 1))
        nc.vector.tensor_scalar(z2_rows[:, 0, :], b_ps[0][:], gi_signed[:, 0:1], None, ALU.mult)
        for t in range(1, PACK):
            scaled_on_scalar(z2_rows[:, t, :], b_ps[t][:], gi_signed[:, t : t + 1])
        z_grouped = sb("z_grouped", [P, PACK, P, PACK], BF16)
        nc.vector.tensor_tensor(
            z_grouped[:].rearrange("p r m t -> p m t r"),
            sums[0][:].rearrange("p t (m r) -> p m t r", r=PACK),
            sums[1][:].rearrange("p t (m r) -> p m t r", r=PACK),
            ALU.max,
        )
        z2_grouped = [sb("z2_grouped%d" % h, [P, HALF, PACK], BF16) for h in range(2)]
        for h in range(2):
            interleave(nc.scalar.copy, z2_grouped[h][:], z2_rows[:, :, h * HALF : (h + 1) * HALF])
        z_words = sb("z_words", [P, H], U32)
        z_scales = sb("z_scales", [P, H], U8)
        quantize(z_words[:], z_scales[:], z_grouped[:].rearrange("p r m t -> p (r m t)"))
        z2_words = sb("z2_words", [P, H], U32)
        z2_scales = sb("z2_scales", [P, H], U8)
        for h in range(2):
            cols = slice(h * HALF, (h + 1) * HALF)
            quantize(
                z2_words[:, cols], z2_scales[:, cols], z2_grouped[h][:].rearrange("p c t -> p (c t)")
            )

        cv_ps = [bank(PACK + r) for r in range(PACK)]
        for r in range(PACK):
            product(r, cv_ps[r], z_words, z_scales, z2_words, z2_scales)
        cv_rows = [sb("cv_rows%d" % r, [P, H], F32) for r in range(PACK)]
        nc.scalar.activation(cv_rows[0][:], cv_ps[0][:], ACT.Copy, scale=CV_SCALE)
        for r in range(1, PACK):
            nc.vector.tensor_scalar(cv_rows[r][:], cv_ps[r][:], CV_SCALE, None, ALU.mult)

        y_scales = sb("y_scales", [P, H], U8)
        out_rows = out_0.rearrange("(p r) c -> p r c", r=PACK)
        out_words = out_1[0].rearrange("p n r -> p (n r)").bitcast(I32)
        for h in range(2):
            lo, hi = h * HALF, (h + 1) * HALF
            y = sb("y%d" % h, [P, PACK, HALF], F32)
            for r in range(PACK):
                gate = sb("gate%d_%d" % (h, r), [P, HALF], F32, tag="gate%d" % r)
                nc.scalar.activation(
                    gate[:], cv_rows[r][:].indirect(entries(n5_l, lo, hi)), ACT.Sigmoid
                )
                nc.vector.tensor_tensor(y[:, r, :], cv_rows[r][:, lo:hi], gate[:], ALU.mult)
            nc.sync.dma_start(out_rows[:, :, lo:hi], y[:])
            y_words = sb("y_words%d" % h, [P, HALF], U32)
            if h == 0:
                shares = ((0, HALF, nc.vector.tensor_copy),)
            else:
                shares = ((0, HALF // 2, nc.vector.tensor_copy), (HALF // 2, HALF, nc.scalar.copy))
            grouped = []
            for c0, c1, copy in shares:
                y_grouped = sb("y_grouped%d_%d" % (h, c0), [P, c1 - c0, PACK], BF16)
                interleave(copy, y_grouped[:], y[:, :, c0:c1])
                grouped.append(y_grouped)
            for (c0, c1, copy), y_grouped in zip(shares, grouped):
                quantize(
                    y_words[:, c0:c1],
                    y_scales[:, lo + c0 : lo + c1],
                    y_grouped[:].rearrange("p c t -> p (c t)"),
                )
            nc.sync.dma_start(out_words[:, lo:hi], y_words[:].bitcast(I32))
        for q in range(4):
            queue = nc.scalar if q % 2 else nc.sync
            queue.dma_start(
                out_2[0, 4 * q : 4 * q + 4, :].bitcast(I32),
                y_scales[QUADRANT * q : QUADRANT * q + 4, :].bitcast(I32),
            )
